import numpy as np
import ml_dtypes


def mxq(x, axis, fmt="e4m3"):
    dtype, down = {"e4m3": (ml_dtypes.float8_e4m3fn, 7), "e5m2": (ml_dtypes.float8_e5m2, 14)}[fmt]
    v = np.moveaxis(np.asarray(x, np.float32).astype(ml_dtypes.bfloat16).astype(np.float64), axis, -1)
    blocks = v.reshape(v.shape[:-1] + (-1, 32))
    amax = np.abs(blocks).max(-1, keepdims=True)
    byte = np.maximum(np.where(amax > 0, np.frexp(amax)[1] - 1 + 127, 0) - down, 1)
    scale = np.exp2(byte - 127.0)
    codes = (blocks / scale).astype(np.float32).astype(dtype).astype(np.float64)
    return np.moveaxis((codes * scale).reshape(v.shape), -1, axis)


WIDE = False


def mx_kscale(k):
    if not WIDE:
        return np.ones(k)
    levels = np.array([10, -10, 5, -5, 0])
    if k % 512:
        return np.exp2(np.random.permutation(np.resize(levels, k // 32))).repeat(32)
    a = np.empty((k // 512, 16))
    for p in range(k // 512):
        a[p, :8] = np.random.permutation(np.resize(levels, 8))
        for g in range(8):
            far = levels[np.abs(levels - a[p, g]) >= 10]
            a[p, g + 8] = far[np.random.randint(len(far))]
    return np.exp2(a.ravel()).repeat(32)


def f64(x):
    return np.asarray(x).astype(np.float64)


def striped8(idx):
    return np.asarray(idx).reshape(8, -1, 16).transpose(0, 2, 1).reshape(128, -1).astype(np.uint16)


def unstriped8(offs):
    return offs.reshape(8, 16, -1).transpose(0, 2, 1).reshape(8, -1).astype(np.int64)


def pick8(x, idx, run):
    r = np.arange(len(x))
    return x[r[:, None], idx[r % (8 * run) // run]]


E2M1 = np.array([0.0, 0.5, 1.0, 1.5, 2.0, 3.0, 4.0, 6.0, -0.0, -0.5, -1.0, -1.5, -2.0, -3.0, -4.0, -6.0])


def pack_weight(w, fmt):
    k, n = w.shape
    w = f64(np.asarray(w, np.float32).astype(ml_dtypes.bfloat16)).reshape(k // 32, 32, n)
    amax = np.abs(w).max(1)
    if fmt == "e4m3":
        byte = np.frexp(amax)[1] - 1 + 127 - 7
    else:
        mant, ex = np.frexp(amax / 6.0)
        byte = np.where(mant > 0.5, ex, ex - 1) + 127
    byte = np.clip(np.where(amax > 0, byte, 1), 1, 254)
    scaled = (w * np.exp2(127.0 - byte)[:, None, :]).reshape(k, n).astype(np.float32)
    by_word = np.ascontiguousarray(scaled.reshape(k // 512, 128, 4, n).transpose(0, 1, 3, 2))
    if fmt == "e4m3":
        words = by_word.astype(ml_dtypes.float8_e4m3fn).view(np.uint8)
    else:
        c = by_word.astype(ml_dtypes.float4_e2m1fn).view(np.uint8) & 0xF
        words = (c[..., 0::2] | (c[..., 1::2] << 4)).reshape(k // 512, 128, 2 * n)
    return np.ascontiguousarray(words), np.ascontiguousarray(byte.astype(np.uint8).reshape(k // 512, 16, n))


def unpack_weight(words, scales, fmt):
    g, _, n = scales.shape
    words = np.ascontiguousarray(words).reshape(g, 128, n, -1)
    if fmt == "e4m3":
        vals = words.view(ml_dtypes.float8_e4m3fn).astype(np.float64)
    else:
        nib = np.empty((g, 128, n, 4), np.uint8)
        nib[..., 0::2] = words & 0xF
        nib[..., 1::2] = words >> 4
        vals = E2M1[nib]
    vals = vals * np.repeat(np.exp2(scales.astype(np.float64) - 127.0), 8, axis=1)[..., None]
    return vals.transpose(0, 1, 3, 2).reshape(g * 512, n)


D, T, U, I, Q = 512, 1024, 1024, 512, 128


def setup_inputs():
    n = np.random.standard_normal
    idx = np.stack([np.random.permutation(T)[:I] for _ in range(8)])
    idx2 = np.stack([np.random.permutation(U)[:I] for _ in range(8)])
    idx3 = np.stack([np.random.permutation(U)[:I] for _ in range(8)])
    idx4 = np.stack([np.random.permutation(U)[:I] for _ in range(8)])
    idx5 = np.stack([np.random.permutation(T)[:I] for _ in range(8)])
    idx6 = np.stack([np.random.permutation(T)[:I] for _ in range(8)])
    fd = mx_kscale(D)
    keysp = pack_weight(n((D, T)) / fd[:, None], "e2m1")
    notesp = pack_weight(n((D, U)) / fd[:, None], "e4m3")
    return {
        "query": (n((D, Q)) * 1.0 / np.sqrt(D) * fd[:, None]).astype(np.float32),
        "keys_words": keysp[0],
        "keys_scales": keysp[1],
        "notes_words": notesp[0],
        "notes_scales": notesp[1],
        "offs": striped8(idx),
        "offs2": striped8(idx2),
        "offs3": striped8(idx3),
        "offs4": striped8(idx4),
        "offs5": striped8(idx5),
        "offs6": striped8(idx6),
    }


def reference(query, keys_words, keys_scales, notes_words, notes_scales, offs, offs2, offs3, offs4, offs5, offs6):
    idx = unstriped8(offs)
    idx2 = unstriped8(offs2)
    idx3 = unstriped8(offs3)
    idx4 = unstriped8(offs4)
    idx5 = unstriped8(offs5)
    idx6 = unstriped8(offs6)
    keysu = unpack_weight(keys_words, keys_scales, "e2m1")
    notesu = unpack_weight(notes_words, notes_scales, "e4m3")
    queryq = mxq(f64(query), 0, "e4m3")
    a = queryq.T @ keysu
    b = queryq.T @ notesu
    f1 = np.zeros((Q, U))
    f1[np.arange(Q)[:, None], idx2[np.arange(Q) % 128 // 16]] = pick8(a, idx, 16)
    w = np.maximum(pick8(f1, idx3, 16), pick8(b, idx4, 16))
    f2 = np.zeros((Q, T))
    f2[np.arange(Q)[:, None], idx5[np.arange(Q) % 128 // 16]] = w
    cc = a + f2
    y = pick8(cc, idx6, 16)
    return y

@@ -1,0 +1,136 @@
+from contextlib import ExitStack
+
+import concourse.mybir as mybir
+
+D, T, U, SLOTS, Q = 512, 1024, 1024, 512, 128
+FLOPS = 2 * D * Q * (T + U)
+
+F32 = mybir.dt.float32
+BF16 = mybir.dt.bfloat16
+I32 = mybir.dt.int32
+U32 = mybir.dt.uint32
+U16 = mybir.dt.uint16
+U8 = mybir.dt.uint8
+FP8X4 = mybir.dt.float8_e4m3fn_x4
+FP4X4 = mybir.dt.float4_e2m1fn_x4
+COPY = mybir.ActivationFunctionType.Copy
+MAX = mybir.AluOpType.max
+ADD = mybir.AluOpType.add
+
+P = 128
+PACK = 4
+LANES = 16
+HALF = SLOTS // 2
+TOKEN_CHUNKS = (256, 256, 256, 128, 128)
+NOTE_CHUNK = 512
+
+
+def load_scales(nc, plane, scales):
+    for quad in range(4):
+        nc.sync.dma_start(
+            out=plane[32 * quad : 32 * quad + 4, :].bitcast(I32),
+            in_=scales[0, 4 * quad : 4 * quad + 4, :].bitcast(I32),
+        )
+
+
+def gather_halves(nc, dst, window, offsets):
+    cols = HALF // LANES
+    nc.vector.tensor_copy(dst[:, :HALF], window[:].indirect(offsets[:, :cols]))
+    nc.scalar.activation(dst[:, HALF:], window[:].indirect(offsets[:, cols:]), COPY)
+
+
+def tile_attend_returned_two_kernel(
+    tc, query, keys_words, keys_scales, notes_words, notes_scales, offs, offs2, offs3, offs4, offs5, offs6, out
+):
+    nc = tc.nc
+    with ExitStack() as ctx:
+        sb = ctx.enter_context(tc.tile_pool(name="sb", bufs=1))
+        psum = ctx.enter_context(tc.psum_pool(name="psum", bufs=1))
+
+        lists = [sb.tile([P, SLOTS // LANES], U16, name=f"list{n}") for n in range(6)]
+        q_raw = sb.tile([P, PACK, Q], F32)
+        q_bf = sb.tile([P, Q, PACK], BF16, align_bytes=64)
+        q_codes = sb.tile([P, Q], U32, align_bytes=64)
+        q_plane = sb.tile([P, Q], U8, align_bytes=64)
+        k_codes = sb.tile([P, 2 * T], U8, align_bytes=64)
+        k_plane = sb.tile([P, T], U8, align_bytes=64)
+        n_codes = sb.tile([P, U], U32, align_bytes=64)
+        n_plane = sb.tile([P, U], U8, align_bytes=64)
+        a = sb.tile([P, T], F32)
+        b = sb.tile([P, U], F32)
+        f1 = sb.tile([P, U], F32)
+        f2 = sb.tile([P, T], F32)
+        cc = sb.tile([P, T], F32)
+        a_picked = sb.tile([P, SLOTS], F32)
+        b_picked = sb.tile([P, SLOTS], F32)
+        f1_picked = sb.tile([P, SLOTS], F32)
+        w = sb.tile([P, SLOTS], F32)
+        y = sb.tile([P, SLOTS], F32)
+
+        nc.vector.memset(k_plane[:].bitcast(I32), 0)
+        nc.vector.memset(n_plane[:].bitcast(I32), 0)
+        nc.vector.memset(f1[:], 0.0)
+        nc.vector.memset(f2[:], 0.0)
+
+        nc.sync.dma_start(out=q_raw[:], in_=query.rearrange("(p j) q -> p j q", j=PACK))
+        nc.sync.dma_start(out=k_codes[:].bitcast(I32), in_=keys_words[0].bitcast(I32))
+        load_scales(nc, k_plane, keys_scales)
+        nc.sync.dma_start(lists[0][:], offs)
+        nc.sync.dma_start(lists[1][:], offs2)
+        load_scales(nc, n_plane, notes_scales)
+        nc.sync.dma_start(
+            out=n_codes[:].bitcast(I32), in_=notes_words[0].rearrange("p n t -> p (n t)").bitcast(I32)
+        )
+        nc.sync.dma_start(lists[3][:], offs4)
+        nc.sync.dma_start(lists[2][:], offs3)
+        nc.sync.dma_start(lists[4][:], offs5)
+        nc.sync.dma_start(lists[5][:], offs6)
+
+        nc.vector.tensor_copy(out=q_bf[:], in_=q_raw[:].rearrange("p j q -> p q j"))
+        nc.vector.quantize_mx(
+            out=q_codes[:].bitcast(FP8X4), scales=q_plane[:], in_=q_bf[:].rearrange("p q j -> p (q j)")
+        )
+
+        start = 0
+        for n, width in enumerate(TOKEN_CHUNKS):
+            bank = psum.tile([P, width], F32, name=f"a_bank{n}")
+            nc.tensor.matmul_mx(
+                out=bank[:],
+                lhsT=q_codes[:].bitcast(FP8X4),
+                lhsT_scale=q_plane[:],
+                rhs=k_codes[:, 2 * start : 2 * (start + width)].bitcast(FP4X4),
+                rhs_scale=k_plane[:, start : start + width],
+                start=True,
+                stop=True,
+            )
+            if n % 2 == 0:
+                nc.scalar.activation(a[:, start : start + width], bank[:], COPY)
+            else:
+                nc.vector.tensor_copy(a[:, start : start + width], bank[:])
+            start = start + width
+
+        gather_halves(nc, a_picked, a, lists[0])
+        nc.vector.tensor_copy(f1[:].indirect(lists[1][:]), a_picked[:])
+
+        for n in range(U // NOTE_CHUNK):
+            cols = slice(n * NOTE_CHUNK, (n + 1) * NOTE_CHUNK)
+            bank = psum.tile([P, NOTE_CHUNK], F32, name=f"b_bank{n}")
+            nc.tensor.matmul_mx(
+                out=bank[:],
+                lhsT=q_codes[:].bitcast(FP8X4),
+                lhsT_scale=q_plane[:],
+                rhs=n_codes[:, cols].bitcast(FP8X4),
+                rhs_scale=n_plane[:, cols],
+                start=True,
+                stop=True,
+            )
+            nc.scalar.activation(b[:, cols], bank[:], COPY)
+        nc.scalar.activation(b_picked[:], b[:].indirect(lists[3][:]), COPY)
+
+        gather_halves(nc, f1_picked, f1, lists[2])
+        nc.vector.tensor_tensor(w[:], f1_picked[:], b_picked[:], MAX)
+        nc.vector.tensor_copy(f2[:].indirect(lists[4][:]), w[:])
+        nc.vector.tensor_tensor(cc[:], a[:], f2[:], ADD)
+        gather_halves(nc, y, cc, lists[5])
+        nc.sync.dma_start(out=out[:, :HALF], in_=y[:, :HALF])
+        nc.scalar.dma_start(out=out[:, HALF:], in_=y[:, HALF:])

@@ -56,42 +56,44 @@ def tile_attend_returned_two_kernel(
         k_plane = sb.tile([P, T], U8, align_bytes=64)
         n_codes = sb.tile([P, U], U32, align_bytes=64)
         n_plane = sb.tile([P, U], U8, align_bytes=64)
-        a = sb.tile([P, T], F32)
-        b = sb.tile([P, U], F32)
+        a = sb.tile([P, T], F32, tag="scores")
         f1 = sb.tile([P, U], F32)
         f2 = sb.tile([P, T], F32)
         cc = sb.tile([P, T], F32)
         a_picked = sb.tile([P, SLOTS], F32)
         b_picked = sb.tile([P, SLOTS], F32)
-        f1_picked = sb.tile([P, SLOTS], F32)
         w = sb.tile([P, SLOTS], F32)
         y = sb.tile([P, SLOTS], F32)
 
         nc.vector.memset(k_plane[:].bitcast(I32), 0)
         nc.vector.memset(n_plane[:].bitcast(I32), 0)
         nc.vector.memset(f1[:], 0.0)
-        nc.vector.memset(f2[:], 0.0)
+        nc.gpsimd.memset(f2[:], 0.0)
 
         nc.sync.dma_start(out=q_raw[:], in_=query.rearrange("(p j) q -> p j q", j=PACK))
         nc.sync.dma_start(out=k_codes[:].bitcast(I32), in_=keys_words[0].bitcast(I32))
         load_scales(nc, k_plane, keys_scales)
         nc.sync.dma_start(lists[0][:], offs)
-        nc.sync.dma_start(lists[1][:], offs2)
-        load_scales(nc, n_plane, notes_scales)
         nc.sync.dma_start(
             out=n_codes[:].bitcast(I32), in_=notes_words[0].rearrange("p n t -> p (n t)").bitcast(I32)
         )
+        nc.sync.dma_start(lists[1][:], offs2)
+        load_scales(nc, n_plane, notes_scales)
         nc.sync.dma_start(lists[3][:], offs4)
         nc.sync.dma_start(lists[2][:], offs3)
         nc.sync.dma_start(lists[4][:], offs5)
         nc.sync.dma_start(lists[5][:], offs6)
 
-        nc.vector.tensor_copy(out=q_bf[:], in_=q_raw[:].rearrange("p j q -> p q j"))
+        nc.vector.tensor_copy(
+            out=q_bf[:].rearrange("p (c i) j -> p c j i", i=4),
+            in_=q_raw[:].rearrange("p j (c i) -> p c j i", i=4),
+        )
         nc.vector.quantize_mx(
             out=q_codes[:].bitcast(FP8X4), scales=q_plane[:], in_=q_bf[:].rearrange("p q j -> p (q j)")
         )
 
         start = 0
+        a_banks = []
         for n, width in enumerate(TOKEN_CHUNKS):
             bank = psum.tile([P, width], F32, name=f"a_bank{n}")
             nc.tensor.matmul_mx(
@@ -107,11 +109,13 @@ def tile_attend_returned_two_kernel(
                 nc.scalar.activation(a[:, start : start + width], bank[:], COPY)
             else:
                 nc.vector.tensor_copy(a[:, start : start + width], bank[:])
+            a_banks.append((bank, slice(start, start + width)))
             start = start + width
 
         gather_halves(nc, a_picked, a, lists[0])
         nc.vector.tensor_copy(f1[:].indirect(lists[1][:]), a_picked[:])
 
+        b = sb.tile([P, U], F32, tag="scores")
         for n in range(U // NOTE_CHUNK):
             cols = slice(n * NOTE_CHUNK, (n + 1) * NOTE_CHUNK)
             bank = psum.tile([P, NOTE_CHUNK], F32, name=f"b_bank{n}")
@@ -127,10 +131,12 @@ def tile_attend_returned_two_kernel(
             nc.scalar.activation(b[:, cols], bank[:], COPY)
         nc.scalar.activation(b_picked[:], b[:].indirect(lists[3][:]), COPY)
 
+        f1_picked = sb.tile([P, SLOTS], F32, tag="scores")
         gather_halves(nc, f1_picked, f1, lists[2])
         nc.vector.tensor_tensor(w[:], f1_picked[:], b_picked[:], MAX)
         nc.vector.tensor_copy(f2[:].indirect(lists[4][:]), w[:])
-        nc.vector.tensor_tensor(cc[:], a[:], f2[:], ADD)
+        for bank, cols in a_banks:
+            nc.vector.tensor_tensor(cc[:, cols], bank[:], f2[:, cols], ADD)
         gather_halves(nc, y, cc, lists[5])
         nc.sync.dma_start(out=out[:, :HALF], in_=y[:, :HALF])
         nc.scalar.dma_start(out=out[:, HALF:], in_=y[:, HALF:])

@@ -23,11 +23,12 @@ LANES = 16
 HALF = SLOTS // 2
 TOKEN_CHUNKS = (256, 256, 256, 128, 128)
 NOTE_CHUNK = 512
+SPLIT = 704
 
 
-def load_scales(nc, plane, scales):
+def load_scales(queues, plane, scales):
     for quad in range(4):
-        nc.sync.dma_start(
+        queues[quad % len(queues)].dma_start(
             out=plane[32 * quad : 32 * quad + 4, :].bitcast(I32),
             in_=scales[0, 4 * quad : 4 * quad + 4, :].bitcast(I32),
         )
@@ -49,7 +50,7 @@ def tile_attend_returned_two_kernel(
 
         lists = [sb.tile([P, SLOTS // LANES], U16, name=f"list{n}") for n in range(6)]
         q_raw = sb.tile([P, PACK, Q], F32)
-        q_bf = sb.tile([P, Q, PACK], BF16, align_bytes=64)
+        q_bf = [sb.tile([P, Q // 2, PACK], BF16, align_bytes=64, name=f"q_bf{n}") for n in range(2)]
         q_codes = sb.tile([P, Q], U32, align_bytes=64)
         q_plane = sb.tile([P, Q], U8, align_bytes=64)
         k_codes = sb.tile([P, 2 * T], U8, align_bytes=64)
@@ -61,7 +62,7 @@ def tile_attend_returned_two_kernel(
         f2 = sb.tile([P, T], F32)
         cc = sb.tile([P, T], F32)
         a_picked = sb.tile([P, SLOTS], F32)
-        b_picked = sb.tile([P, SLOTS], F32)
+        b_picked = sb.tile([P, SLOTS], F32, tag="spare")
         w = sb.tile([P, SLOTS], F32)
         y = sb.tile([P, SLOTS], F32)
 
@@ -72,25 +73,34 @@ def tile_attend_returned_two_kernel(
 
         nc.sync.dma_start(out=q_raw[:], in_=query.rearrange("(p j) q -> p j q", j=PACK))
         nc.sync.dma_start(out=k_codes[:].bitcast(I32), in_=keys_words[0].bitcast(I32))
-        load_scales(nc, k_plane, keys_scales)
+        load_scales((nc.sync,), k_plane, keys_scales)
         nc.sync.dma_start(lists[0][:], offs)
         nc.sync.dma_start(
             out=n_codes[:].bitcast(I32), in_=notes_words[0].rearrange("p n t -> p (n t)").bitcast(I32)
         )
         nc.sync.dma_start(lists[1][:], offs2)
-        load_scales(nc, n_plane, notes_scales)
+        load_scales((nc.sync,), n_plane, notes_scales)
         nc.sync.dma_start(lists[3][:], offs4)
         nc.sync.dma_start(lists[2][:], offs3)
         nc.sync.dma_start(lists[4][:], offs5)
         nc.sync.dma_start(lists[5][:], offs6)
 
+        q_halves = (slice(0, Q // 2), slice(Q // 2, Q))
+        nc.scalar.activation(
+            q_bf[0][:].rearrange("p (c i) j -> p c j i", i=4),
+            q_raw[:, :, q_halves[0]].rearrange("p j (c i) -> p c j i", i=4),
+            COPY,
+        )
         nc.vector.tensor_copy(
-            out=q_bf[:].rearrange("p (c i) j -> p c j i", i=4),
-            in_=q_raw[:].rearrange("p j (c i) -> p c j i", i=4),
+            out=q_bf[1][:].rearrange("p (c i) j -> p c j i", i=4),
+            in_=q_raw[:, :, q_halves[1]].rearrange("p j (c i) -> p c j i", i=4),
         )
-        nc.vector.quantize_mx(
-            out=q_codes[:].bitcast(FP8X4), scales=q_plane[:], in_=q_bf[:].rearrange("p q j -> p (q j)")
-        )
+        for n, cols in enumerate(q_halves):
+            nc.vector.quantize_mx(
+                out=q_codes[:, cols].bitcast(FP8X4),
+                scales=q_plane[:, cols],
+                in_=q_bf[n][:].rearrange("p q j -> p (q j)"),
+            )
 
         start = 0
         a_banks = []
@@ -133,10 +143,21 @@ def tile_attend_returned_two_kernel(
 
         f1_picked = sb.tile([P, SLOTS], F32, tag="scores")
         gather_halves(nc, f1_picked, f1, lists[2])
-        nc.vector.tensor_tensor(w[:], f1_picked[:], b_picked[:], MAX)
+        for cols in (slice(HALF, SLOTS), slice(0, HALF)):
+            nc.vector.tensor_tensor(w[:, cols], f1_picked[:, cols], b_picked[:, cols], MAX)
         nc.vector.tensor_copy(f2[:].indirect(lists[4][:]), w[:])
+        a_tail = sb.tile([P, T - SPLIT], F32, tag="spare")
         for bank, cols in a_banks:
-            nc.vector.tensor_tensor(cc[:, cols], bank[:], f2[:, cols], ADD)
+            low = max(cols.start, SPLIT)
+            if low < cols.stop:
+                nc.scalar.activation(a_tail[:, low - SPLIT : cols.stop - SPLIT], bank[:, low - cols.start :], COPY)
+        for bank, cols in a_banks:
+            high = min(cols.stop, SPLIT)
+            if cols.start < high:
+                nc.vector.tensor_tensor(
+                    cc[:, cols.start : high], bank[:, : high - cols.start], f2[:, cols.start : high], ADD
+                )
+        nc.gpsimd.tensor_tensor(cc[:, SPLIT:], a_tail[:], f2[:, SPLIT:], ADD)
         gather_halves(nc, y, cc, lists[5])
         nc.sync.dma_start(out=out[:, :HALF], in_=y[:, :HALF])
         nc.scalar.dma_start(out=out[:, HALF:], in_=y[:, HALF:])

@@ -50,7 +50,7 @@ def tile_attend_returned_two_kernel(
 
         lists = [sb.tile([P, SLOTS // LANES], U16, name=f"list{n}") for n in range(6)]
         q_raw = sb.tile([P, PACK, Q], F32)
-        q_bf = [sb.tile([P, Q // 2, PACK], BF16, align_bytes=64, name=f"q_bf{n}") for n in range(2)]
+        q_bf = [sb.tile([P, Q // 2, PACK], BF16, align_bytes=64, name=f"q_bf{n}", tag=f"q_bf{n}") for n in range(2)]
         q_codes = sb.tile([P, Q], U32, align_bytes=64)
         q_plane = sb.tile([P, Q], U8, align_bytes=64)
         k_codes = sb.tile([P, 2 * T], U8, align_bytes=64)
@@ -59,7 +59,6 @@ def tile_attend_returned_two_kernel(
         n_plane = sb.tile([P, U], U8, align_bytes=64)
         a = sb.tile([P, T], F32, tag="scores")
         f1 = sb.tile([P, U], F32)
-        f2 = sb.tile([P, T], F32)
         cc = sb.tile([P, T], F32)
         a_picked = sb.tile([P, SLOTS], F32)
         b_picked = sb.tile([P, SLOTS], F32, tag="spare")
@@ -69,16 +68,15 @@ def tile_attend_returned_two_kernel(
         nc.vector.memset(k_plane[:].bitcast(I32), 0)
         nc.vector.memset(n_plane[:].bitcast(I32), 0)
         nc.vector.memset(f1[:], 0.0)
-        nc.gpsimd.memset(f2[:], 0.0)
 
         nc.sync.dma_start(out=q_raw[:], in_=query.rearrange("(p j) q -> p j q", j=PACK))
         nc.sync.dma_start(out=k_codes[:].bitcast(I32), in_=keys_words[0].bitcast(I32))
         load_scales((nc.sync,), k_plane, keys_scales)
         nc.sync.dma_start(lists[0][:], offs)
+        nc.sync.dma_start(lists[1][:], offs2)
         nc.sync.dma_start(
             out=n_codes[:].bitcast(I32), in_=notes_words[0].rearrange("p n t -> p (n t)").bitcast(I32)
         )
-        nc.sync.dma_start(lists[1][:], offs2)
         load_scales((nc.sync,), n_plane, notes_scales)
         nc.sync.dma_start(lists[3][:], offs4)
         nc.sync.dma_start(lists[2][:], offs3)
@@ -101,6 +99,9 @@ def tile_attend_returned_two_kernel(
                 scales=q_plane[:, cols],
                 in_=q_bf[n][:].rearrange("p q j -> p (q j)"),
             )
+
+        f2 = sb.tile([P, T], F32, align_bytes=64, tag="q_bf1")
+        nc.gpsimd.memset(f2[:], 0.0)
 
         start = 0
         a_banks = []

from contextlib import ExitStack

import concourse.mybir as mybir

D, T, U, SLOTS, Q = 512, 1024, 1024, 512, 128
FLOPS = 2 * D * Q * (T + U)

F32 = mybir.dt.float32
BF16 = mybir.dt.bfloat16
I32 = mybir.dt.int32
U32 = mybir.dt.uint32
U16 = mybir.dt.uint16
U8 = mybir.dt.uint8
FP8X4 = mybir.dt.float8_e4m3fn_x4
FP4X4 = mybir.dt.float4_e2m1fn_x4
COPY = mybir.ActivationFunctionType.Copy
MAX = mybir.AluOpType.max
ADD = mybir.AluOpType.add

P = 128
PACK = 4
LANES = 16
HALF = SLOTS // 2
TOKEN_CHUNKS = (256, 256, 256, 128, 128)
NOTE_CHUNK = 512
SPLIT = 704


def load_scales(queues, plane, scales):
    for quad in range(4):
        queues[quad % len(queues)].dma_start(
            out=plane[32 * quad : 32 * quad + 4, :].bitcast(I32),
            in_=scales[0, 4 * quad : 4 * quad + 4, :].bitcast(I32),
        )


def gather_halves(nc, dst, window, offsets):
    cols = HALF // LANES
    nc.vector.tensor_copy(dst[:, :HALF], window[:].indirect(offsets[:, :cols]))
    nc.scalar.activation(dst[:, HALF:], window[:].indirect(offsets[:, cols:]), COPY)


def tile_attend_returned_two_kernel(
    tc, query, keys_words, keys_scales, notes_words, notes_scales, offs, offs2, offs3, offs4, offs5, offs6, out
):
    nc = tc.nc
    with ExitStack() as ctx:
        sb = ctx.enter_context(tc.tile_pool(name="sb", bufs=1))
        psum = ctx.enter_context(tc.psum_pool(name="psum", bufs=1))

        lists = [sb.tile([P, SLOTS // LANES], U16, name=f"list{n}") for n in range(6)]
        q_raw = sb.tile([P, PACK, Q], F32)
        q_bf = [sb.tile([P, Q // 2, PACK], BF16, align_bytes=64, name=f"q_bf{n}", tag=f"q_bf{n}") for n in range(2)]
        q_codes = sb.tile([P, Q], U32, align_bytes=64)
        q_plane = sb.tile([P, Q], U8, align_bytes=64)
        k_codes = sb.tile([P, 2 * T], U8, align_bytes=64)
        k_plane = sb.tile([P, T], U8, align_bytes=64)
        n_codes = sb.tile([P, U], U32, align_bytes=64)
        n_plane = sb.tile([P, U], U8, align_bytes=64)
        a = sb.tile([P, T], F32, tag="scores")
        f1 = sb.tile([P, U], F32)
        cc = sb.tile([P, T], F32)
        a_picked = sb.tile([P, SLOTS], F32)
        b_picked = sb.tile([P, SLOTS], F32, tag="spare")
        w = sb.tile([P, SLOTS], F32)
        y = sb.tile([P, SLOTS], F32)

        nc.vector.memset(k_plane[:].bitcast(I32), 0)
        nc.vector.memset(n_plane[:].bitcast(I32), 0)
        nc.vector.memset(f1[:], 0.0)

        nc.sync.dma_start(out=q_raw[:], in_=query.rearrange("(p j) q -> p j q", j=PACK))
        nc.sync.dma_start(out=k_codes[:].bitcast(I32), in_=keys_words[0].bitcast(I32))
        load_scales((nc.sync,), k_plane, keys_scales)
        nc.sync.dma_start(lists[0][:], offs)
        nc.sync.dma_start(lists[1][:], offs2)
        nc.sync.dma_start(
            out=n_codes[:].bitcast(I32), in_=notes_words[0].rearrange("p n t -> p (n t)").bitcast(I32)
        )
        load_scales((nc.sync,), n_plane, notes_scales)
        nc.sync.dma_start(lists[3][:], offs4)
        nc.sync.dma_start(lists[2][:], offs3)
        nc.sync.dma_start(lists[4][:], offs5)
        nc.sync.dma_start(lists[5][:], offs6)

        q_halves = (slice(0, Q // 2), slice(Q // 2, Q))
        nc.scalar.activation(
            q_bf[0][:].rearrange("p (c i) j -> p c j i", i=4),
            q_raw[:, :, q_halves[0]].rearrange("p j (c i) -> p c j i", i=4),
            COPY,
        )
        nc.vector.tensor_copy(
            out=q_bf[1][:].rearrange("p (c i) j -> p c j i", i=4),
            in_=q_raw[:, :, q_halves[1]].rearrange("p j (c i) -> p c j i", i=4),
        )
        for n, cols in enumerate(q_halves):
            nc.vector.quantize_mx(
                out=q_codes[:, cols].bitcast(FP8X4),
                scales=q_plane[:, cols],
                in_=q_bf[n][:].rearrange("p q j -> p (q j)"),
            )

        f2 = sb.tile([P, T], F32, align_bytes=64, tag="q_bf1")
        nc.gpsimd.memset(f2[:], 0.0)

        start = 0
        a_banks = []
        for n, width in enumerate(TOKEN_CHUNKS):
            bank = psum.tile([P, width], F32, name=f"a_bank{n}")
            nc.tensor.matmul_mx(
                out=bank[:],
                lhsT=q_codes[:].bitcast(FP8X4),
                lhsT_scale=q_plane[:],
                rhs=k_codes[:, 2 * start : 2 * (start + width)].bitcast(FP4X4),
                rhs_scale=k_plane[:, start : start + width],
                start=True,
                stop=True,
            )
            if n % 2 == 0:
                nc.scalar.activation(a[:, start : start + width], bank[:], COPY)
            else:
                nc.vector.tensor_copy(a[:, start : start + width], bank[:])
            a_banks.append((bank, slice(start, start + width)))
            start = start + width

        gather_halves(nc, a_picked, a, lists[0])
        nc.vector.tensor_copy(f1[:].indirect(lists[1][:]), a_picked[:])

        b = sb.tile([P, U], F32, tag="scores")
        for n in range(U // NOTE_CHUNK):
            cols = slice(n * NOTE_CHUNK, (n + 1) * NOTE_CHUNK)
            bank = psum.tile([P, NOTE_CHUNK], F32, name=f"b_bank{n}")
            nc.tensor.matmul_mx(
                out=bank[:],
                lhsT=q_codes[:].bitcast(FP8X4),
                lhsT_scale=q_plane[:],
                rhs=n_codes[:, cols].bitcast(FP8X4),
                rhs_scale=n_plane[:, cols],
                start=True,
                stop=True,
            )
            nc.scalar.activation(b[:, cols], bank[:], COPY)
        nc.scalar.activation(b_picked[:], b[:].indirect(lists[3][:]), COPY)

        f1_picked = sb.tile([P, SLOTS], F32, tag="scores")
        gather_halves(nc, f1_picked, f1, lists[2])
        for cols in (slice(HALF, SLOTS), slice(0, HALF)):
            nc.vector.tensor_tensor(w[:, cols], f1_picked[:, cols], b_picked[:, cols], MAX)
        nc.vector.tensor_copy(f2[:].indirect(lists[4][:]), w[:])
        a_tail = sb.tile([P, T - SPLIT], F32, tag="spare")
        for bank, cols in a_banks:
            low = max(cols.start, SPLIT)
            if low < cols.stop:
                nc.scalar.activation(a_tail[:, low - SPLIT : cols.stop - SPLIT], bank[:, low - cols.start :], COPY)
        for bank, cols in a_banks:
            high = min(cols.stop, SPLIT)
            if cols.start < high:
                nc.vector.tensor_tensor(
                    cc[:, cols.start : high], bank[:, : high - cols.start], f2[:, cols.start : high], ADD
                )
        nc.gpsimd.tensor_tensor(cc[:, SPLIT:], a_tail[:], f2[:, SPLIT:], ADD)
        gather_halves(nc, y, cc, lists[5])
        nc.sync.dma_start(out=out[:, :HALF], in_=y[:, :HALF])
        nc.scalar.dma_start(out=out[:, HALF:], in_=y[:, HALF:])
